import numpy as np
import ml_dtypes


def mxq(x, axis, fmt="e4m3"):
    dtype, down = {"e4m3": (ml_dtypes.float8_e4m3fn, 7), "e5m2": (ml_dtypes.float8_e5m2, 14)}[fmt]
    v = np.moveaxis(np.asarray(x, np.float32).astype(ml_dtypes.bfloat16).astype(np.float64), axis, -1)
    blocks = v.reshape(v.shape[:-1] + (-1, 32))
    amax = np.abs(blocks).max(-1, keepdims=True)
    byte = np.maximum(np.where(amax > 0, np.frexp(amax)[1] - 1 + 127, 0) - down, 1)
    scale = np.exp2(byte - 127.0)
    codes = (blocks / scale).astype(np.float32).astype(dtype).astype(np.float64)
    return np.moveaxis((codes * scale).reshape(v.shape), -1, axis)


WIDE = False


def mx_kscale(k):
    if not WIDE:
        return np.ones(k)
    levels = np.array([10, -10, 5, -5, 0])
    if k % 512:
        return np.exp2(np.random.permutation(np.resize(levels, k // 32))).repeat(32)
    a = np.empty((k // 512, 16))
    for p in range(k // 512):
        a[p, :8] = np.random.permutation(np.resize(levels, 8))
        for g in range(8):
            far = levels[np.abs(levels - a[p, g]) >= 10]
            a[p, g + 8] = far[np.random.randint(len(far))]
    return np.exp2(a.ravel()).repeat(32)


def f64(x):
    return np.asarray(x).astype(np.float64)


def striped(idx):
    return np.tile(idx.reshape(-1, 16).T, (8, 1)).astype(np.uint16)


def unstriped(offs):
    return offs[:16].T.reshape(-1).astype(np.int64)


E2M1 = np.array([0.0, 0.5, 1.0, 1.5, 2.0, 3.0, 4.0, 6.0, -0.0, -0.5, -1.0, -1.5, -2.0, -3.0, -4.0, -6.0])


def pack_weight(w, fmt):
    k, n = w.shape
    w = f64(np.asarray(w, np.float32).astype(ml_dtypes.bfloat16)).reshape(k // 32, 32, n)
    amax = np.abs(w).max(1)
    if fmt == "e4m3":
        byte = np.frexp(amax)[1] - 1 + 127 - 7
    else:
        mant, ex = np.frexp(amax / 6.0)
        byte = np.where(mant > 0.5, ex, ex - 1) + 127
    byte = np.clip(np.where(amax > 0, byte, 1), 1, 254)
    scaled = (w * np.exp2(127.0 - byte)[:, None, :]).reshape(k, n).astype(np.float32)
    by_word = np.ascontiguousarray(scaled.reshape(k // 512, 128, 4, n).transpose(0, 1, 3, 2))
    if fmt == "e4m3":
        words = by_word.astype(ml_dtypes.float8_e4m3fn).view(np.uint8)
    else:
        c = by_word.astype(ml_dtypes.float4_e2m1fn).view(np.uint8) & 0xF
        words = (c[..., 0::2] | (c[..., 1::2] << 4)).reshape(k // 512, 128, 2 * n)
    return np.ascontiguousarray(words), np.ascontiguousarray(byte.astype(np.uint8).reshape(k // 512, 16, n))


def unpack_weight(words, scales, fmt):
    g, _, n = scales.shape
    words = np.ascontiguousarray(words).reshape(g, 128, n, -1)
    if fmt == "e4m3":
        vals = words.view(ml_dtypes.float8_e4m3fn).astype(np.float64)
    else:
        nib = np.empty((g, 128, n, 4), np.uint8)
        nib[..., 0::2] = words & 0xF
        nib[..., 1::2] = words >> 4
        vals = E2M1[nib]
    vals = vals * np.repeat(np.exp2(scales.astype(np.float64) - 127.0), 8, axis=1)[..., None]
    return vals.transpose(0, 1, 3, 2).reshape(g * 512, n)


def gelu(v):
    return 0.5 * v * (1.0 + np.tanh(np.sqrt(2.0 / np.pi) * (v + 0.044715 * v**3)))


def striped8(idx):
    return np.concatenate([v.reshape(-1, 16).T for v in idx]).astype(np.uint16)


def unstriped8(offs):
    return np.stack([offs[16 * g:16 * g + 16].T.reshape(-1) for g in range(8)]).astype(np.int64)


def put_heads(h, wgs, idx8, t2):
    r = np.arange(h.shape[0])
    page = np.zeros((h.shape[0], t2))
    page[r[:, None], idx8[r % 512 // 64]] = wgs[r // 4 % 128] * h
    return page


K, H, N, T, S, T2, P, G, R = 1024, 1024, 512, 4096, 1024, 2048, 1024, 8, 16

def setup_inputs():
    n = np.random.standard_normal
    s = mx_kscale(K)[:, None]
    u = mx_kscale(H)[:, None]
    tab_words, tab_scales = pack_weight(n((K, T)) * s, "e4m3")
    wf_words, wf_scales = pack_weight(n((K, H)) / np.sqrt(K) / s, "e2m1")
    slots = np.stack([np.random.permutation(T2)[:S] for _ in range(G)])
    return {
        "tab_words": tab_words, "tab_scales": tab_scales,
        "offs": striped(np.random.permutation(T)[:S]),
        "w1": (n((K, H)) / np.sqrt(K) / s).astype(np.float32),
        "wf_words": wf_words, "wf_scales": wf_scales,
        "wgs": np.repeat(np.random.uniform(0.5, 2.0, (G, S)), R, axis=0).astype(np.float32),
        "offs2": striped8(slots),
        "offs3": striped(np.random.permutation(T2)[:P]),
        "ground": (0.8 * n((H, P))).astype(np.float32),
        "gain": (np.exp(0.3 * n(H)) * u[:, 0]).astype(np.float32),
        "w2": (n((H, N)) / np.sqrt(H) / u).astype(np.float32),
        "bias": (0.5 * n(N)).astype(np.float32),
    }

def reference(tab_words, tab_scales, offs, w1, wf_words, wf_scales, wgs, offs2, offs3, ground, gain, w2, bias):
    v = unpack_weight(tab_words, tab_scales, "e4m3")[:, unstriped(offs)]
    wf = unpack_weight(wf_words, wf_scales, "e2m1")
    near = mxq(f64(w1), 0, "e4m3").T @ v
    far = wf.T @ v
    h = np.maximum(near, far)
    page = put_heads(h, f64(wgs), unstriped8(offs2), T2)
    x = page[:, unstriped(offs3)]
    z = np.tanh(x + f64(ground)) * f64(gain)[:, None]
    y = mxq(f64(w2), 0, "e4m3").T @ mxq(z, 0, "e4m3")
    return y + f64(bias)[:, None]

@@ -1,0 +1,291 @@
+from contextlib import ExitStack
+
+import concourse.mybir as mybir
+from concourse.masks import make_identity
+
+K, H, N, T, S, T2, M = 1024, 1024, 512, 4096, 1024, 2048, 1024
+FLOPS = 2 * 2 * K * H * S + 2 * H * N * M
+
+F32 = mybir.dt.float32
+BF16 = mybir.dt.bfloat16
+I32 = mybir.dt.int32
+U32 = mybir.dt.uint32
+U16 = mybir.dt.uint16
+U8 = mybir.dt.uint8
+FP8X4 = mybir.dt.float8_e4m3fn_x4
+FP4X4 = mybir.dt.float4_e2m1fn_x4
+ALU = mybir.AluOpType
+ACT = mybir.ActivationFunctionType
+
+P = 128
+PACK = 4
+PASS = P * PACK
+BANK = 512
+SLICES = 8
+QUARTER = 256
+PE_SLICES = 0
+
+
+def tile_list_bumper_echo_slots_kernel(
+    tc, tab_words, tab_scales, offs, w1, wf_words, wf_scales, wgs, offs2, offs3, ground, gain, w2, bias, out
+):
+    nc = tc.nc
+    with ExitStack() as ctx:
+        lists = ctx.enter_context(tc.tile_pool(name="lists", bufs=1))
+        keep = ctx.enter_context(tc.tile_pool(name="keep", bufs=1))
+        big = ctx.enter_context(tc.tile_pool(name="big", bufs=3))
+        ring = ctx.enter_context(tc.tile_pool(name="ring", bufs=2))
+        psum = ctx.enter_context(tc.psum_pool(name="psum", bufs=1))
+
+        idx = lists.tile([P, S // 16], U16, name="idx")
+        idx2 = lists.tile([P, S // 16], U16, name="idx2")
+        idx3 = lists.tile([P, M // 16], U16, name="idx3")
+
+        tab_sc = keep.tile([P, 2, T], U8, name="tab_sc", align_bytes=64)
+        wf_sc_raw = keep.tile([P, 2 * H], U8, name="wf_sc_raw", align_bytes=64)
+        nc.vector.memset(tab_sc[:].rearrange("p a t -> p (a t)").bitcast(I32), 0)
+        nc.vector.memset(wf_sc_raw[:].bitcast(I32), 0)
+
+        tab_w = [big.tile([P, T], I32, name="tab_w%d" % a, tag="big", align_bytes=64) for a in range(2)]
+        nc.sync.dma_start(idx[:], offs)
+        nc.sync.dma_start(idx2[:], offs2)
+        nc.sync.dma_start(idx3[:], offs3)
+        gain_sb = keep.tile([P, 2, PACK], F32, name="gain_sb")
+        nc.scalar.dma_start(out=gain_sb[:], in_=gain.rearrange("(b p i) -> p b i", b=2, i=PACK))
+        bias_sb = keep.tile([P, N // P], F32, name="bias_sb")
+        with nc.allow_non_contiguous_dma("bias one element a partition"):
+            nc.scalar.dma_start(out=bias_sb[:], in_=bias.rearrange("(t p) -> p t", p=P))
+        for q in range(4):
+            nc.gpsimd.dma_start(
+                out=tab_sc[32 * q : 32 * q + 4, :, :].bitcast(I32),
+                in_=tab_scales[:, 4 * q : 4 * q + 4, :].rearrange("a r t -> r a t").bitcast(I32),
+            )
+        for q in range(4):
+            nc.scalar.dma_start(
+                out=wf_sc_raw[32 * q : 32 * q + 4, :].bitcast(I32).rearrange("r (a t) -> r a t", a=2),
+                in_=wf_scales[:, 4 * q : 4 * q + 4, :].rearrange("a r t -> r a t").bitcast(I32),
+            )
+        wf_raw = keep.tile([P, 4 * H], U8, name="wf_raw", align_bytes=64)
+        nc.sync.dma_start(out=wf_raw[:].bitcast(I32).rearrange("p (a c) -> p a c", a=2), in_=wf_words.rearrange("a p c -> p a c").bitcast(I32))
+
+        def load_weight(src):
+            raw = ring.tile([P, PACK, PASS], F32, name="w_raw", tag="w_raw", bufs=3)
+            nc.sync.dma_start(out=raw[:], in_=src.rearrange("(p j) c -> p j c", j=PACK))
+            return raw
+
+        def quantise(grouped, name):
+            width = grouped.shape[1]
+            codes = keep.tile([P, width], U32, name=name + "_codes", align_bytes=64)
+            scales = keep.tile([P, width], U8, name=name + "_scales", align_bytes=64)
+            nc.vector.quantize_mx(
+                out=codes[:].bitcast(FP8X4), scales=scales[:], in_=grouped[:].rearrange("p c j -> p (c j)")
+            )
+            return codes, scales
+
+        def quantise_w1(raw, name):
+            grouped = ring.tile([P, PASS, PACK], BF16, name="w_grouped", tag="w_grouped", align_bytes=64)
+            nc.scalar.copy(
+                out=grouped[:].rearrange("p (i q) j -> p q i j", i=PACK),
+                in_=raw[:].rearrange("p j (q i) -> p q i j", i=PACK),
+            )
+            return quantise(grouped, name)
+
+        def quantise_w2(raw, name):
+            grouped = ring.tile([P, PASS, PACK], BF16, name="w_grouped", tag="w_grouped", align_bytes=64)
+            nc.scalar.copy(out=grouped[:], in_=raw[:].rearrange("p j c -> p c j"))
+            return quantise(grouped, name)
+
+        def w1_block(a, b):
+            return w1[a * PASS : (a + 1) * PASS, b * PASS : (b + 1) * PASS]
+
+        w1_raw = {}
+        for a in range(2):
+            w1_raw[a, 0] = load_weight(w1_block(a, 0))
+        for a in range(2):
+            nc.sync.dma_start(out=tab_w[a][:], in_=tab_words[a].rearrange("p t i -> p (t i)").bitcast(I32))
+        wgs_sb = keep.tile([P, S], F32, name="wgs_sb")
+        nc.sync.dma_start(out=wgs_sb[:], in_=wgs)
+        ground_sb = {}
+
+        def load_ground(b):
+            ground_sb[b] = big.tile([P, PACK, M], F32, name="ground%d" % b, tag="big", align_bytes=64)
+            nc.sync.dma_start(
+                out=ground_sb[b][:], in_=ground[b * PASS : (b + 1) * PASS, :].rearrange("(p i) m -> p i m", i=PACK)
+            )
+
+        load_ground(0)
+
+        pages = [keep.tile([P, T2], F32, name="page%d" % u, align_bytes=64) for u in range(2)]
+        for page in pages:
+            nc.vector.memset(page[:], 0.0)
+
+
+        wf_w = keep.tile([P, 4, PACK, 2 * P], U8, name="wf_w", align_bytes=64)
+        wf_sc = keep.tile([P, 4, PACK, P], U8, name="wf_sc", align_bytes=64)
+        nc.vector.tensor_copy(
+            out=wf_w[:].bitcast(U16),
+            in_=wf_raw[:].bitcast(U16).rearrange("p (g q i) -> p g i q", g=4, i=PACK),
+        )
+        nc.vector.tensor_copy(
+            out=wf_sc[:], in_=wf_sc_raw[:].rearrange("p (g q i) -> p g i q", g=4, i=PACK)
+        )
+
+        v_w = [keep.tile([P, S], U32, name="v_w%d" % a, align_bytes=64) for a in range(2)]
+        v_sc = [keep.tile([P, S], U8, name="v_sc%d" % a, align_bytes=64) for a in range(2)]
+        for a in range(2):
+            nc.vector.tensor_copy(v_sc[a][:], tab_sc[:, a, :].indirect(idx[:]))
+        w1_q = {}
+        for a in range(2):
+            w1_q[a, 0] = quantise_w1(w1_raw[a, 0], "w1_%d0" % a)
+        nc.vector.tensor_copy(v_w[0][:], tab_w[0][:].bitcast(U32).indirect(idx[:]))
+        for half in range(2):
+            nc.vector.tensor_copy(
+                v_w[1][:, half * BANK : (half + 1) * BANK],
+                tab_w[1][:].bitcast(U32).indirect(idx[:, half * 32 : (half + 1) * 32]),
+            )
+
+        for a in range(2):
+            w1_raw[a, 1] = load_weight(w1_block(a, 1))
+        load_ground(1)
+
+        def bank(tag):
+            return psum.tile([P, BANK], F32, name=tag, tag=tag, bufs=8)
+
+        h_sb = {}
+
+        def responses(s):
+            b, i = divmod(s, PACK)
+            h_sb[s] = ring.tile([P, S], F32, name="h", tag="h", bufs=3)
+            for half in range(2):
+                cols = slice(half * BANK, (half + 1) * BANK)
+                near = bank("acc")
+                far = bank("acc")
+                for a in range(2):
+                    codes, scales = w1_q[a, b]
+                    nc.tensor.matmul_mx(
+                        out=near[:],
+                        lhsT=codes[:, i * P : (i + 1) * P].bitcast(FP8X4),
+                        lhsT_scale=scales[:, i * P : (i + 1) * P],
+                        rhs=v_w[a][:, cols].bitcast(FP8X4),
+                        rhs_scale=v_sc[a][:, cols],
+                        start=(a == 0),
+                        stop=(a == 1),
+                    )
+                for a in range(2):
+                    nc.tensor.matmul_mx(
+                        out=far[:],
+                        lhsT=wf_w[:, 2 * a + b, i, :].bitcast(FP4X4),
+                        lhsT_scale=wf_sc[:, 2 * a + b, i, :],
+                        rhs=v_w[a][:, cols].bitcast(FP8X4),
+                        rhs_scale=v_sc[a][:, cols],
+                        start=(a == 0),
+                        stop=(a == 1),
+                    )
+                near_sb = ring.tile([P, BANK], F32, name="near_sb", tag="near_sb", bufs=3)
+                nc.scalar.copy(out=near_sb[:], in_=near[:])
+                nc.vector.tensor_tensor(h_sb[s][:, cols], far[:], near_sb[:], ALU.max)
+
+        def place(s, parts):
+            width = S // parts
+            for part in range(parts):
+                cols = slice(part * width, (part + 1) * width)
+                nc.vector.tensor_tensor(
+                    pages[s % 2][:].indirect(idx2[:, part * width // 16 : (part + 1) * width // 16]),
+                    h_sb[s][:, cols],
+                    wgs_sb[:, cols],
+                    ALU.mult,
+                )
+
+        z_grouped = [keep.tile([P, M, PACK], BF16, name="z_grouped%d" % b, align_bytes=64) for b in range(2)]
+
+        def fetch_fused(s, start, width):
+            b, i = divmod(s, PACK)
+            cols = slice(start, start + width)
+            x = ring.tile([P, width], F32, name="x", tag="x")
+            nc.vector.tensor_tensor(
+                x[:],
+                pages[s % 2][:].indirect(idx3[:, start // 16 : (start + width) // 16]),
+                ground_sb[b][:, i, cols],
+                ALU.add,
+            )
+            bounded = ring.tile([P, width], F32, name="bounded", tag="bounded")
+            nc.scalar.activation(bounded[:], x[:], ACT.Tanh)
+            nc.scalar.activation(z_grouped[b][:, cols, i], bounded[:], ACT.Copy, scale=gain_sb[:, b, i : i + 1])
+
+        z_codes = [keep.tile([P, M], U32, name="z_codes%d" % b, align_bytes=64) for b in range(2)]
+        z_sc = [keep.tile([P, M], U8, name="z_sc%d" % b, align_bytes=64) for b in range(2)]
+
+        def quantise_z(b, start, width):
+            cols = slice(start, start + width)
+            nc.vector.quantize_mx(
+                out=z_codes[b][:, cols].bitcast(FP8X4),
+                scales=z_sc[b][:, cols],
+                in_=z_grouped[b][:, cols, :].rearrange("p c j -> p (c j)"),
+            )
+
+        w2_q = {}
+        responses(0)
+        responses(1)
+        for s in range(SLICES - 1):
+            place(s, 2 if s == 0 else 1)
+            if s < 2:
+                w1_q[s, 1] = quantise_w1(w1_raw[s, 1], "w1_%d1" % s)
+            if s + 2 < SLICES:
+                responses(s + 2)
+            if s < PE_SLICES:
+                fetch_fused(s, 0, M)
+            else:
+                fetch_fused(s, 0, M)
+            if s in (2, 3):
+                b = s - 2
+                w2_q[b] = quantise_w2(load_weight(w2[b * PASS : (b + 1) * PASS, :]), "w2_%d" % b)
+            if s == 4:
+                quantise_z(0, 0, M)
+        place(SLICES - 1, 1)
+
+        def product_pass(acc, b, quarter, pair):
+            cols = slice(quarter * QUARTER, (quarter + 1) * QUARTER)
+            codes, scales = w2_q[b]
+            for u in range(2):
+                t = 2 * pair + u
+                nc.tensor.matmul_mx(
+                    out=acc[:, u * QUARTER : (u + 1) * QUARTER],
+                    lhsT=codes[:, t * P : (t + 1) * P].bitcast(FP8X4),
+                    lhsT_scale=scales[:, t * P : (t + 1) * P],
+                    rhs=z_codes[b][:, cols].bitcast(FP8X4),
+                    rhs_scale=z_sc[b][:, cols],
+                    start=(b == 0 and u == 0),
+                    stop=(b == 1 and u == 1),
+                )
+
+        y = {}
+        for quarter in range(4):
+            for pair in range(2):
+                y[quarter, pair] = bank("acc")
+                product_pass(y[quarter, pair], 0, quarter, pair)
+
+        staged = big.tile([P, 4, 4, QUARTER], F32, name="staged", tag="big", align_bytes=64)
+        out_view = out.rearrange("(t p) m -> p t m", p=P)
+        for quarter in range(4):
+            fetch_fused(SLICES - 1, quarter * QUARTER, QUARTER)
+        for quarter in range(4):
+            cols = slice(quarter * QUARTER, (quarter + 1) * QUARTER)
+            quantise_z(1, quarter * QUARTER, QUARTER)
+            for pair in range(2):
+                acc = y[quarter, pair]
+                product_pass(acc, 1, quarter, pair)
+                for u in range(2):
+                    t = 2 * pair + u
+                    if pair == 1 and quarter >= 2:
+                        nc.scalar.activation(
+                            staged[:, quarter, t, :], acc[:, u * QUARTER : (u + 1) * QUARTER], ACT.Identity,
+                            bias=bias_sb[:, t : t + 1],
+                        )
+                    else:
+                        nc.vector.tensor_scalar(
+                            staged[:, quarter, t, :], acc[:, u * QUARTER : (u + 1) * QUARTER],
+                            bias_sb[:, t : t + 1], None, ALU.add,
+                        )
+                nc.sync.dma_start(
+                    out=out_view[:, 2 * pair : 2 * pair + 2, cols], in_=staged[:, quarter, 2 * pair : 2 * pair + 2, :]
+                )

@@ -1,7 +1,6 @@
 from contextlib import ExitStack
 
 import concourse.mybir as mybir
-from concourse.masks import make_identity
 
 K, H, N, T, S, T2, M = 1024, 1024, 512, 4096, 1024, 2048, 1024
 FLOPS = 2 * 2 * K * H * S + 2 * H * N * M
@@ -23,7 +22,9 @@ PASS = P * PACK
 BANK = 512
 SLICES = 8
 QUARTER = 256
-PE_SLICES = 0
+GROUP = 16
+FIRST_RUNS = ((0, 256), (256, 256), (512, 512))
+RUNS = ((0, 512), (512, 512))
 
 
 def tile_list_bumper_echo_slots_kernel(
@@ -33,50 +34,49 @@ def tile_list_bumper_echo_slots_kernel(
     with ExitStack() as ctx:
         lists = ctx.enter_context(tc.tile_pool(name="lists", bufs=1))
         keep = ctx.enter_context(tc.tile_pool(name="keep", bufs=1))
-        big = ctx.enter_context(tc.tile_pool(name="big", bufs=3))
         ring = ctx.enter_context(tc.tile_pool(name="ring", bufs=2))
-        psum = ctx.enter_context(tc.psum_pool(name="psum", bufs=1))
+        psum = ctx.enter_context(tc.psum_pool(name="psum", bufs=8))
 
-        idx = lists.tile([P, S // 16], U16, name="idx")
-        idx2 = lists.tile([P, S // 16], U16, name="idx2")
-        idx3 = lists.tile([P, M // 16], U16, name="idx3")
+        idx = lists.tile([P, S // GROUP], U16, name="idx")
+        idx2 = lists.tile([P, S // GROUP], U16, name="idx2")
+        idx3 = lists.tile([P, M // GROUP], U16, name="idx3")
 
-        tab_sc = keep.tile([P, 2, T], U8, name="tab_sc", align_bytes=64)
+        def entries(index_list, start, width):
+            return index_list[:, start // GROUP : (start + width) // GROUP]
+
+        tab_sc = keep.tile([P, T], U8, name="tab_sc", align_bytes=64)
         wf_sc_raw = keep.tile([P, 2 * H], U8, name="wf_sc_raw", align_bytes=64)
-        nc.vector.memset(tab_sc[:].rearrange("p a t -> p (a t)").bitcast(I32), 0)
+        v_sc = [keep.tile([P, S], U8, name="v_sc%d" % a, align_bytes=64) for a in range(2)]
+        nc.vector.memset(tab_sc[:].bitcast(I32), 0)
         nc.vector.memset(wf_sc_raw[:].bitcast(I32), 0)
-
-        tab_w = [big.tile([P, T], I32, name="tab_w%d" % a, tag="big", align_bytes=64) for a in range(2)]
-        nc.sync.dma_start(idx[:], offs)
-        nc.sync.dma_start(idx2[:], offs2)
-        nc.sync.dma_start(idx3[:], offs3)
-        gain_sb = keep.tile([P, 2, PACK], F32, name="gain_sb")
-        nc.scalar.dma_start(out=gain_sb[:], in_=gain.rearrange("(b p i) -> p b i", b=2, i=PACK))
-        bias_sb = keep.tile([P, N // P], F32, name="bias_sb")
-        with nc.allow_non_contiguous_dma("bias one element a partition"):
-            nc.scalar.dma_start(out=bias_sb[:], in_=bias.rearrange("(t p) -> p t", p=P))
-        for q in range(4):
-            nc.gpsimd.dma_start(
-                out=tab_sc[32 * q : 32 * q + 4, :, :].bitcast(I32),
-                in_=tab_scales[:, 4 * q : 4 * q + 4, :].rearrange("a r t -> r a t").bitcast(I32),
-            )
-        for q in range(4):
-            nc.scalar.dma_start(
-                out=wf_sc_raw[32 * q : 32 * q + 4, :].bitcast(I32).rearrange("r (a t) -> r a t", a=2),
-                in_=wf_scales[:, 4 * q : 4 * q + 4, :].rearrange("a r t -> r a t").bitcast(I32),
-            )
-        wf_raw = keep.tile([P, 4 * H], U8, name="wf_raw", align_bytes=64)
-        nc.sync.dma_start(out=wf_raw[:].bitcast(I32).rearrange("p (a c) -> p a c", a=2), in_=wf_words.rearrange("a p c -> p a c").bitcast(I32))
+        nc.vector.memset(v_sc[1][:].bitcast(I32), 0)
+        pages = [keep.tile([P, T2], F32, name="page%d" % u, align_bytes=64) for u in range(2)]
+        for page in pages:
+            nc.gpsimd.memset(page[:], 0.0)
 
         def load_weight(src):
-            raw = ring.tile([P, PACK, PASS], F32, name="w_raw", tag="w_raw", bufs=3)
+            raw = ring.tile([P, PACK, PASS], F32, name="w_raw", tag="w_raw")
             nc.sync.dma_start(out=raw[:], in_=src.rearrange("(p j) c -> p j c", j=PACK))
             return raw
 
+        def load_w1(a, b):
+            return load_weight(w1[a * PASS : (a + 1) * PASS, b * PASS : (b + 1) * PASS])
+
+        def load_table(a):
+            words = ring.tile([P, T], I32, name="tab_w", tag="big", align_bytes=64)
+            nc.sync.dma_start(out=words[:], in_=tab_words[a].rearrange("p t i -> p (t i)").bitcast(I32))
+            return words
+
+        def load_ground(b):
+            rows = ring.tile([P, PACK, M], F32, name="ground_sb", tag="big", align_bytes=64)
+            nc.sync.dma_start(
+                out=rows[:], in_=ground[b * PASS : (b + 1) * PASS, :].rearrange("(p i) m -> p i m", i=PACK)
+            )
+            return rows
+
         def quantise(grouped, name):
-            width = grouped.shape[1]
-            codes = keep.tile([P, width], U32, name=name + "_codes", align_bytes=64)
-            scales = keep.tile([P, width], U8, name=name + "_scales", align_bytes=64)
+            codes = keep.tile([P, PASS], U32, name=name + "_codes", align_bytes=64)
+            scales = keep.tile([P, PASS], U8, name=name + "_scales", align_bytes=64)
             nc.vector.quantize_mx(
                 out=codes[:].bitcast(FP8X4), scales=scales[:], in_=grouped[:].rearrange("p c j -> p (c j)")
             )
@@ -95,71 +95,74 @@ def tile_list_bumper_echo_slots_kernel(
             nc.scalar.copy(out=grouped[:], in_=raw[:].rearrange("p j c -> p c j"))
             return quantise(grouped, name)
 
-        def w1_block(a, b):
-            return w1[a * PASS : (a + 1) * PASS, b * PASS : (b + 1) * PASS]
-
-        w1_raw = {}
-        for a in range(2):
-            w1_raw[a, 0] = load_weight(w1_block(a, 0))
-        for a in range(2):
-            nc.sync.dma_start(out=tab_w[a][:], in_=tab_words[a].rearrange("p t i -> p (t i)").bitcast(I32))
-        wgs_sb = keep.tile([P, S], F32, name="wgs_sb")
-        nc.sync.dma_start(out=wgs_sb[:], in_=wgs)
-        ground_sb = {}
-
-        def load_ground(b):
-            ground_sb[b] = big.tile([P, PACK, M], F32, name="ground%d" % b, tag="big", align_bytes=64)
+        nc.sync.dma_start(idx[:], offs)
+        w1_raw = {(0, 0): load_w1(0, 0)}
+        for q in range(4):
             nc.sync.dma_start(
-                out=ground_sb[b][:], in_=ground[b * PASS : (b + 1) * PASS, :].rearrange("(p i) m -> p i m", i=PACK)
+                out=tab_sc[32 * q : 32 * q + 8, :].bitcast(I32),
+                in_=tab_scales[:, 4 * q : 4 * q + 4, :].bitcast(I32),
             )
+        tab_w = [load_table(0)]
+        wf_raw = keep.tile([P, 4 * H], U8, name="wf_raw", align_bytes=64)
+        nc.sync.dma_start(
+            out=wf_raw[:].bitcast(I32).rearrange("p (a c) -> p a c", a=2),
+            in_=wf_words.rearrange("a p c -> p a c").bitcast(I32),
+        )
+        for q in range(4):
+            nc.sync.dma_start(
+                out=wf_sc_raw[32 * q : 32 * q + 4, :].bitcast(I32).rearrange("r (a t) -> r a t", a=2),
+                in_=wf_scales[:, 4 * q : 4 * q + 4, :].rearrange("a r t -> r a t").bitcast(I32),
+            )
+        w1_raw[1, 0] = load_w1(1, 0)
+        tab_w.append(load_table(1))
+        wgs_sb = keep.tile([P, S], F32, name="wgs_sb")
+        nc.sync.dma_start(idx2[:], offs2)
+        nc.sync.dma_start(out=wgs_sb[:], in_=wgs)
+        nc.sync.dma_start(idx3[:], offs3)
+        gain_sb = keep.tile([P, 2, PACK], F32, name="gain_sb")
+        nc.sync.dma_start(out=gain_sb[:], in_=gain.rearrange("(b p i) -> p b i", b=2, i=PACK))
+        bias_sb = keep.tile([P, N // P], F32, name="bias_sb")
+        with nc.allow_non_contiguous_dma("bias one element a partition"):
+            nc.sync.dma_start(out=bias_sb[:], in_=bias.rearrange("(t p) -> p t", p=P))
 
-        load_ground(0)
-
-        pages = [keep.tile([P, T2], F32, name="page%d" % u, align_bytes=64) for u in range(2)]
-        for page in pages:
-            nc.vector.memset(page[:], 0.0)
-
-
+        v_w = [keep.tile([P, S], U32, name="v_w%d" % a, align_bytes=64) for a in range(2)]
+        nc.vector.tensor_copy(v_sc[0][:], tab_sc[:].indirect(idx[:]))
+        nc.gpsimd.dma_start(out=v_sc[1][0 : P - 4, :].bitcast(I32), in_=v_sc[0][4:P, :].bitcast(I32))
+        w1_q = {(0, 0): quantise_w1(w1_raw[0, 0], "w1_00")}
+        nc.vector.tensor_copy(v_w[0][:], tab_w[0][:].bitcast(U32).indirect(idx[:]))
         wf_w = keep.tile([P, 4, PACK, 2 * P], U8, name="wf_w", align_bytes=64)
         wf_sc = keep.tile([P, 4, PACK, P], U8, name="wf_sc", align_bytes=64)
         nc.vector.tensor_copy(
             out=wf_w[:].bitcast(U16),
             in_=wf_raw[:].bitcast(U16).rearrange("p (g q i) -> p g i q", g=4, i=PACK),
         )
-        nc.vector.tensor_copy(
-            out=wf_sc[:], in_=wf_sc_raw[:].rearrange("p (g q i) -> p g i q", g=4, i=PACK)
-        )
-
-        v_w = [keep.tile([P, S], U32, name="v_w%d" % a, align_bytes=64) for a in range(2)]
-        v_sc = [keep.tile([P, S], U8, name="v_sc%d" % a, align_bytes=64) for a in range(2)]
-        for a in range(2):
-            nc.vector.tensor_copy(v_sc[a][:], tab_sc[:, a, :].indirect(idx[:]))
-        w1_q = {}
-        for a in range(2):
-            w1_q[a, 0] = quantise_w1(w1_raw[a, 0], "w1_%d0" % a)
-        nc.vector.tensor_copy(v_w[0][:], tab_w[0][:].bitcast(U32).indirect(idx[:]))
-        for half in range(2):
+        nc.vector.tensor_copy(out=wf_sc[:], in_=wf_sc_raw[:].rearrange("p (g q i) -> p g i q", g=4, i=PACK))
+        w1_q[1, 0] = quantise_w1(w1_raw[1, 0], "w1_10")
+        for start, width in RUNS:
             nc.vector.tensor_copy(
-                v_w[1][:, half * BANK : (half + 1) * BANK],
-                tab_w[1][:].bitcast(U32).indirect(idx[:, half * 32 : (half + 1) * 32]),
+                v_w[1][:, start : start + width], tab_w[1][:].bitcast(U32).indirect(entries(idx, start, width))
             )
 
-        for a in range(2):
-            w1_raw[a, 1] = load_weight(w1_block(a, 1))
-        load_ground(1)
+        w1_raw[0, 1] = load_w1(0, 1)
+        ground_sb = [load_ground(0)]
+        w1_raw[1, 1] = load_w1(1, 1)
+        ground_sb.append(load_ground(1))
 
-        def bank(tag):
-            return psum.tile([P, BANK], F32, name=tag, tag=tag, bufs=8)
+        def ground_rows(s):
+            return ground_sb[s // PACK][:, s % PACK, :]
 
-        h_sb = {}
+        h_first = [keep.tile([P, S], F32, name="h_first%d" % s) for s in range(2)]
 
-        def responses(s):
+        def h_rows(s):
+            return h_first[s][:] if s < 2 else ground_rows(s - 2)
+
+        def products(s, runs):
             b, i = divmod(s, PACK)
-            h_sb[s] = ring.tile([P, S], F32, name="h", tag="h", bufs=3)
-            for half in range(2):
-                cols = slice(half * BANK, (half + 1) * BANK)
-                near = bank("acc")
-                far = bank("acc")
+            made = []
+            for start, width in runs:
+                cols = slice(start, start + width)
+                near = psum.tile([P, width], F32, name="near", tag="bank")
+                far = psum.tile([P, width], F32, name="far", tag="bank")
                 for a in range(2):
                     codes, scales = w1_q[a, b]
                     nc.tensor.matmul_mx(
@@ -181,33 +184,30 @@ def tile_list_bumper_echo_slots_kernel(
                         start=(a == 0),
                         stop=(a == 1),
                     )
-                near_sb = ring.tile([P, BANK], F32, name="near_sb", tag="near_sb", bufs=3)
+                near_sb = ring.tile([P, width], F32, name="near_sb", tag="near_sb", bufs=4)
                 nc.scalar.copy(out=near_sb[:], in_=near[:])
-                nc.vector.tensor_tensor(h_sb[s][:, cols], far[:], near_sb[:], ALU.max)
+                made.append((start, width, near_sb, far))
+            return made
 
-        def place(s, parts):
-            width = S // parts
-            for part in range(parts):
-                cols = slice(part * width, (part + 1) * width)
-                nc.vector.tensor_tensor(
-                    pages[s % 2][:].indirect(idx2[:, part * width // 16 : (part + 1) * width // 16]),
-                    h_sb[s][:, cols],
-                    wgs_sb[:, cols],
-                    ALU.mult,
-                )
+        def stronger(s, start, width, near_sb, far):
+            nc.vector.tensor_tensor(h_rows(s)[:, start : start + width], far[:], near_sb[:], ALU.max)
+
+        def place(s, start, width):
+            cols = slice(start, start + width)
+            nc.vector.tensor_tensor(
+                pages[s % 2][:].indirect(entries(idx2, start, width)), h_rows(s)[:, cols], wgs_sb[:, cols], ALU.mult
+            )
 
         z_grouped = [keep.tile([P, M, PACK], BF16, name="z_grouped%d" % b, align_bytes=64) for b in range(2)]
 
-        def fetch_fused(s, start, width):
+        def fetch(s, start, width):
             b, i = divmod(s, PACK)
             cols = slice(start, start + width)
-            x = ring.tile([P, width], F32, name="x", tag="x")
+            x = ring.tile([P, width], F32, name="x", tag="x", bufs=4)
             nc.vector.tensor_tensor(
-                x[:],
-                pages[s % 2][:].indirect(idx3[:, start // 16 : (start + width) // 16]),
-                ground_sb[b][:, i, cols],
-                ALU.add,
+                x[:], pages[s % 2][:].indirect(entries(idx3, start, width)), ground_rows(s)[:, cols], ALU.add
             )
+
             bounded = ring.tile([P, width], F32, name="bounded", tag="bounded")
             nc.scalar.activation(bounded[:], x[:], ACT.Tanh)
             nc.scalar.activation(z_grouped[b][:, cols, i], bounded[:], ACT.Copy, scale=gain_sb[:, b, i : i + 1])
@@ -223,25 +223,28 @@ def tile_list_bumper_echo_slots_kernel(
                 in_=z_grouped[b][:, cols, :].rearrange("p c j -> p (c j)"),
             )
 
+
         w2_q = {}
-        responses(0)
-        responses(1)
-        for s in range(SLICES - 1):
-            place(s, 2 if s == 0 else 1)
+        made = products(0, FIRST_RUNS)
+        for s in range(SLICES):
+            ahead = products(s + 1, RUNS) if s + 1 < SLICES else None
+            if s == 0:
+                for run in made:
+                    stronger(s, *run)
+                    place(s, run[0], run[1])
+            else:
+                for run in made:
+                    stronger(s, *run)
+                fetch(s - 1, 0, M)
+                place(s, 0, S)
+            made = ahead
             if s < 2:
                 w1_q[s, 1] = quantise_w1(w1_raw[s, 1], "w1_%d1" % s)
-            if s + 2 < SLICES:
-                responses(s + 2)
-            if s < PE_SLICES:
-                fetch_fused(s, 0, M)
-            else:
-                fetch_fused(s, 0, M)
-            if s in (2, 3):
-                b = s - 2
+            if s in (4, 5):
+                b = s - 4
                 w2_q[b] = quantise_w2(load_weight(w2[b * PASS : (b + 1) * PASS, :]), "w2_%d" % b)
-            if s == 4:
+            if s == 5:
                 quantise_z(0, 0, M)
-        place(SLICES - 1, 1)
 
         def product_pass(acc, b, quarter, pair):
             cols = slice(quarter * QUARTER, (quarter + 1) * QUARTER)
@@ -261,31 +264,29 @@ def tile_list_bumper_echo_slots_kernel(
         y = {}
         for quarter in range(4):
             for pair in range(2):
-                y[quarter, pair] = bank("acc")
+                y[quarter, pair] = psum.tile([P, BANK], F32, name="y", tag="bank")
                 product_pass(y[quarter, pair], 0, quarter, pair)
 
-        staged = big.tile([P, 4, 4, QUARTER], F32, name="staged", tag="big", align_bytes=64)
         out_view = out.rearrange("(t p) m -> p t m", p=P)
         for quarter in range(4):
-            fetch_fused(SLICES - 1, quarter * QUARTER, QUARTER)
+            fetch(SLICES - 1, quarter * QUARTER, QUARTER)
         for quarter in range(4):
             cols = slice(quarter * QUARTER, (quarter + 1) * QUARTER)
             quantise_z(1, quarter * QUARTER, QUARTER)
             for pair in range(2):
                 acc = y[quarter, pair]
                 product_pass(acc, 1, quarter, pair)
+                staged = keep.tile([P, 2, QUARTER], F32, name="staged%d%d" % (quarter, pair))
                 for u in range(2):
                     t = 2 * pair + u
-                    if pair == 1 and quarter >= 2:
+                    if pair == 1 and quarter >= 1:
                         nc.scalar.activation(
-                            staged[:, quarter, t, :], acc[:, u * QUARTER : (u + 1) * QUARTER], ACT.Identity,
+                            staged[:, u, :], acc[:, u * QUARTER : (u + 1) * QUARTER], ACT.Identity,
                             bias=bias_sb[:, t : t + 1],
                         )
                     else:
                         nc.vector.tensor_scalar(
-                            staged[:, quarter, t, :], acc[:, u * QUARTER : (u + 1) * QUARTER],
+                            staged[:, u, :], acc[:, u * QUARTER : (u + 1) * QUARTER],
                             bias_sb[:, t : t + 1], None, ALU.add,
                         )
-                nc.sync.dma_start(
-                    out=out_view[:, 2 * pair : 2 * pair + 2, cols], in_=staged[:, quarter, 2 * pair : 2 * pair + 2, :]
-                )
+                nc.sync.dma_start(out=out_view[:, 2 * pair : 2 * pair + 2, cols], in_=staged[:])

@@ -35,7 +35,7 @@ def tile_list_bumper_echo_slots_kernel(
         lists = ctx.enter_context(tc.tile_pool(name="lists", bufs=1))
         keep = ctx.enter_context(tc.tile_pool(name="keep", bufs=1))
         ring = ctx.enter_context(tc.tile_pool(name="ring", bufs=2))
-        psum = ctx.enter_context(tc.psum_pool(name="psum", bufs=8))
+        psum = ctx.enter_context(tc.psum_pool(name="psum", bufs=1))
 
         idx = lists.tile([P, S // GROUP], U16, name="idx")
         idx2 = lists.tile([P, S // GROUP], U16, name="idx2")
@@ -52,23 +52,25 @@ def tile_list_bumper_echo_slots_kernel(
         nc.vector.memset(v_sc[1][:].bitcast(I32), 0)
         pages = [keep.tile([P, T2], F32, name="page%d" % u, align_bytes=64) for u in range(2)]
         for page in pages:
-            nc.gpsimd.memset(page[:], 0.0)
+            nc.vector.memset(page[:], 0.0)
 
-        def load_weight(src):
-            raw = ring.tile([P, PACK, PASS], F32, name="w_raw", tag="w_raw")
-            nc.sync.dma_start(out=raw[:], in_=src.rearrange("(p j) c -> p j c", j=PACK))
+        def stage(shape, dtype, name):
+            return ring.tile(shape, dtype, name=name, tag="big", bufs=3, align_bytes=64)
+
+        def load_weight(raw, src):
+            nc.sync.dma_start(out=raw, in_=src.rearrange("(p j) c -> p j c", j=PACK))
             return raw
 
-        def load_w1(a, b):
-            return load_weight(w1[a * PASS : (a + 1) * PASS, b * PASS : (b + 1) * PASS])
+        def load_w1(raw, a, b):
+            return load_weight(raw[:, a, :, :], w1[a * PASS : (a + 1) * PASS, b * PASS : (b + 1) * PASS])
 
         def load_table(a):
-            words = ring.tile([P, T], I32, name="tab_w", tag="big", align_bytes=64)
+            words = stage([P, T], I32, "tab_w")
             nc.sync.dma_start(out=words[:], in_=tab_words[a].rearrange("p t i -> p (t i)").bitcast(I32))
             return words
 
         def load_ground(b):
-            rows = ring.tile([P, PACK, M], F32, name="ground_sb", tag="big", align_bytes=64)
+            rows = stage([P, PACK, M], F32, "ground_sb")
             nc.sync.dma_start(
                 out=rows[:], in_=ground[b * PASS : (b + 1) * PASS, :].rearrange("(p i) m -> p i m", i=PACK)
             )
@@ -86,34 +88,35 @@ def tile_list_bumper_echo_slots_kernel(
             grouped = ring.tile([P, PASS, PACK], BF16, name="w_grouped", tag="w_grouped", align_bytes=64)
             nc.scalar.copy(
                 out=grouped[:].rearrange("p (i q) j -> p q i j", i=PACK),
-                in_=raw[:].rearrange("p j (q i) -> p q i j", i=PACK),
+                in_=raw.rearrange("p j (q i) -> p q i j", i=PACK),
             )
             return quantise(grouped, name)
 
         def quantise_w2(raw, name):
             grouped = ring.tile([P, PASS, PACK], BF16, name="w_grouped", tag="w_grouped", align_bytes=64)
-            nc.scalar.copy(out=grouped[:], in_=raw[:].rearrange("p j c -> p c j"))
+            nc.scalar.copy(out=grouped[:], in_=raw.rearrange("p j c -> p c j"))
             return quantise(grouped, name)
 
         nc.sync.dma_start(idx[:], offs)
-        w1_raw = {(0, 0): load_w1(0, 0)}
-        for q in range(4):
-            nc.sync.dma_start(
-                out=tab_sc[32 * q : 32 * q + 8, :].bitcast(I32),
-                in_=tab_scales[:, 4 * q : 4 * q + 4, :].bitcast(I32),
-            )
-        tab_w = [load_table(0)]
         wf_raw = keep.tile([P, 4 * H], U8, name="wf_raw", align_bytes=64)
         nc.sync.dma_start(
             out=wf_raw[:].bitcast(I32).rearrange("p (a c) -> p a c", a=2),
             in_=wf_words.rearrange("a p c -> p a c").bitcast(I32),
         )
-        for q in range(4):
+        for r in range(4):
             nc.sync.dma_start(
-                out=wf_sc_raw[32 * q : 32 * q + 4, :].bitcast(I32).rearrange("r (a t) -> r a t", a=2),
-                in_=wf_scales[:, 4 * q : 4 * q + 4, :].rearrange("a r t -> r a t").bitcast(I32),
+                out=tab_sc[r:P:16, :].bitcast(I32),
+                in_=tab_scales[:, r:16:4, :].rearrange("a q t -> q a t").bitcast(I32),
             )
-        w1_raw[1, 0] = load_w1(1, 0)
+        w1_first = stage([P, 2, PACK, PASS], F32, "w1_first")
+        w1_raw = {(0, 0): load_w1(w1_first, 0, 0)}
+        w1_raw[1, 0] = load_w1(w1_first, 1, 0)
+        tab_w = [load_table(0)]
+        for r in range(4):
+            nc.sync.dma_start(
+                out=wf_sc_raw[r:P:32, :].bitcast(I32).rearrange("q (a t) -> q a t", a=2),
+                in_=wf_scales[:, r:16:4, :].rearrange("a q t -> q a t").bitcast(I32),
+            )
         tab_w.append(load_table(1))
         wgs_sb = keep.tile([P, S], F32, name="wgs_sb")
         nc.sync.dma_start(idx2[:], offs2)
@@ -127,25 +130,26 @@ def tile_list_bumper_echo_slots_kernel(
 
         v_w = [keep.tile([P, S], U32, name="v_w%d" % a, align_bytes=64) for a in range(2)]
         nc.vector.tensor_copy(v_sc[0][:], tab_sc[:].indirect(idx[:]))
-        nc.gpsimd.dma_start(out=v_sc[1][0 : P - 4, :].bitcast(I32), in_=v_sc[0][4:P, :].bitcast(I32))
+        nc.gpsimd.dma_start(out=v_sc[1][0 : P - 16, :].bitcast(I32), in_=v_sc[0][16:P, :].bitcast(I32))
         w1_q = {(0, 0): quantise_w1(w1_raw[0, 0], "w1_00")}
-        nc.vector.tensor_copy(v_w[0][:], tab_w[0][:].bitcast(U32).indirect(idx[:]))
         wf_w = keep.tile([P, 4, PACK, 2 * P], U8, name="wf_w", align_bytes=64)
         wf_sc = keep.tile([P, 4, PACK, P], U8, name="wf_sc", align_bytes=64)
         nc.vector.tensor_copy(
             out=wf_w[:].bitcast(U16),
             in_=wf_raw[:].bitcast(U16).rearrange("p (g q i) -> p g i q", g=4, i=PACK),
         )
-        nc.vector.tensor_copy(out=wf_sc[:], in_=wf_sc_raw[:].rearrange("p (g q i) -> p g i q", g=4, i=PACK))
         w1_q[1, 0] = quantise_w1(w1_raw[1, 0], "w1_10")
+        nc.vector.tensor_copy(v_w[0][:], tab_w[0][:].bitcast(U32).indirect(idx[:]))
+        nc.vector.tensor_copy(out=wf_sc[:], in_=wf_sc_raw[:].rearrange("p (g q i) -> p g i q", g=4, i=PACK))
         for start, width in RUNS:
             nc.vector.tensor_copy(
                 v_w[1][:, start : start + width], tab_w[1][:].bitcast(U32).indirect(entries(idx, start, width))
             )
 
-        w1_raw[0, 1] = load_w1(0, 1)
         ground_sb = [load_ground(0)]
-        w1_raw[1, 1] = load_w1(1, 1)
+        w1_second = stage([P, 2, PACK, PASS], F32, "w1_second")
+        for a in range(2):
+            w1_raw[a, 1] = load_w1(w1_second, a, 1)
         ground_sb.append(load_ground(1))
 
         def ground_rows(s):
@@ -161,8 +165,8 @@ def tile_list_bumper_echo_slots_kernel(
             made = []
             for start, width in runs:
                 cols = slice(start, start + width)
-                near = psum.tile([P, width], F32, name="near", tag="bank")
-                far = psum.tile([P, width], F32, name="far", tag="bank")
+                near = psum.tile([P, width], F32, name="near", tag="near", bufs=2)
+                far = psum.tile([P, width], F32, name="far", tag="far", bufs=6)
                 for a in range(2):
                     codes, scales = w1_q[a, b]
                     nc.tensor.matmul_mx(
@@ -184,7 +188,7 @@ def tile_list_bumper_echo_slots_kernel(
                         start=(a == 0),
                         stop=(a == 1),
                     )
-                near_sb = ring.tile([P, width], F32, name="near_sb", tag="near_sb", bufs=4)
+                near_sb = ring.tile([P, width], F32, name="near_sb", tag="near_sb", bufs=6)
                 nc.scalar.copy(out=near_sb[:], in_=near[:])
                 made.append((start, width, near_sb, far))
             return made
@@ -225,9 +229,11 @@ def tile_list_bumper_echo_slots_kernel(
 
 
         w2_q = {}
-        made = products(0, FIRST_RUNS)
+        waiting = [products(0, FIRST_RUNS), products(1, RUNS)]
         for s in range(SLICES):
-            ahead = products(s + 1, RUNS) if s + 1 < SLICES else None
+            if s + 2 < SLICES:
+                waiting.append(products(s + 2, RUNS))
+            made = waiting[s]
             if s == 0:
                 for run in made:
                     stronger(s, *run)
@@ -237,12 +243,15 @@ def tile_list_bumper_echo_slots_kernel(
                     stronger(s, *run)
                 fetch(s - 1, 0, M)
                 place(s, 0, S)
-            made = ahead
             if s < 2:
                 w1_q[s, 1] = quantise_w1(w1_raw[s, 1], "w1_%d1" % s)
+            if s == 1:
+                w2_raw = stage([P, 2, PACK, N], F32, "w2_raw")
+                for b in range(2):
+                    load_weight(w2_raw[:, b, :, :], w2[b * PASS : (b + 1) * PASS, :])
             if s in (4, 5):
                 b = s - 4
-                w2_q[b] = quantise_w2(load_weight(w2[b * PASS : (b + 1) * PASS, :]), "w2_%d" % b)
+                w2_q[b] = quantise_w2(w2_raw[:, b, :, :], "w2_%d" % b)
             if s == 5:
                 quantise_z(0, 0, M)
 
@@ -264,7 +273,7 @@ def tile_list_bumper_echo_slots_kernel(
         y = {}
         for quarter in range(4):
             for pair in range(2):
-                y[quarter, pair] = psum.tile([P, BANK], F32, name="y", tag="bank")
+                y[quarter, pair] = psum.tile([P, BANK], F32, name="y", tag="near" if quarter == 0 else "far", bufs=2 if quarter == 0 else 6)
                 product_pass(y[quarter, pair], 0, quarter, pair)
 
         out_view = out.rearrange("(t p) m -> p t m", p=P)

from contextlib import ExitStack

import concourse.mybir as mybir

K, H, N, T, S, T2, M = 1024, 1024, 512, 4096, 1024, 2048, 1024
FLOPS = 2 * 2 * K * H * S + 2 * H * N * M

F32 = mybir.dt.float32
BF16 = mybir.dt.bfloat16
I32 = mybir.dt.int32
U32 = mybir.dt.uint32
U16 = mybir.dt.uint16
U8 = mybir.dt.uint8
FP8X4 = mybir.dt.float8_e4m3fn_x4
FP4X4 = mybir.dt.float4_e2m1fn_x4
ALU = mybir.AluOpType
ACT = mybir.ActivationFunctionType

P = 128
PACK = 4
PASS = P * PACK
BANK = 512
SLICES = 8
QUARTER = 256
GROUP = 16
FIRST_RUNS = ((0, 256), (256, 256), (512, 512))
RUNS = ((0, 512), (512, 512))


def tile_list_bumper_echo_slots_kernel(
    tc, tab_words, tab_scales, offs, w1, wf_words, wf_scales, wgs, offs2, offs3, ground, gain, w2, bias, out
):
    nc = tc.nc
    with ExitStack() as ctx:
        lists = ctx.enter_context(tc.tile_pool(name="lists", bufs=1))
        keep = ctx.enter_context(tc.tile_pool(name="keep", bufs=1))
        ring = ctx.enter_context(tc.tile_pool(name="ring", bufs=2))
        psum = ctx.enter_context(tc.psum_pool(name="psum", bufs=1))

        idx = lists.tile([P, S // GROUP], U16, name="idx")
        idx2 = lists.tile([P, S // GROUP], U16, name="idx2")
        idx3 = lists.tile([P, M // GROUP], U16, name="idx3")

        def entries(index_list, start, width):
            return index_list[:, start // GROUP : (start + width) // GROUP]

        tab_sc = keep.tile([P, T], U8, name="tab_sc", align_bytes=64)
        wf_sc_raw = keep.tile([P, 2 * H], U8, name="wf_sc_raw", align_bytes=64)
        v_sc = [keep.tile([P, S], U8, name="v_sc%d" % a, align_bytes=64) for a in range(2)]
        nc.vector.memset(tab_sc[:].bitcast(I32), 0)
        nc.vector.memset(wf_sc_raw[:].bitcast(I32), 0)
        nc.vector.memset(v_sc[1][:].bitcast(I32), 0)
        pages = [keep.tile([P, T2], F32, name="page%d" % u, align_bytes=64) for u in range(2)]
        for page in pages:
            nc.vector.memset(page[:], 0.0)

        def stage(shape, dtype, name):
            return ring.tile(shape, dtype, name=name, tag="big", bufs=3, align_bytes=64)

        def load_weight(raw, src):
            nc.sync.dma_start(out=raw, in_=src.rearrange("(p j) c -> p j c", j=PACK))
            return raw

        def load_w1(raw, a, b):
            return load_weight(raw[:, a, :, :], w1[a * PASS : (a + 1) * PASS, b * PASS : (b + 1) * PASS])

        def load_table(a):
            words = stage([P, T], I32, "tab_w")
            nc.sync.dma_start(out=words[:], in_=tab_words[a].rearrange("p t i -> p (t i)").bitcast(I32))
            return words

        def load_ground(b):
            rows = stage([P, PACK, M], F32, "ground_sb")
            nc.sync.dma_start(
                out=rows[:], in_=ground[b * PASS : (b + 1) * PASS, :].rearrange("(p i) m -> p i m", i=PACK)
            )
            return rows

        def quantise(grouped, name):
            codes = keep.tile([P, PASS], U32, name=name + "_codes", align_bytes=64)
            scales = keep.tile([P, PASS], U8, name=name + "_scales", align_bytes=64)
            nc.vector.quantize_mx(
                out=codes[:].bitcast(FP8X4), scales=scales[:], in_=grouped[:].rearrange("p c j -> p (c j)")
            )
            return codes, scales

        def quantise_w1(raw, name):
            grouped = ring.tile([P, PASS, PACK], BF16, name="w_grouped", tag="w_grouped", align_bytes=64)
            nc.scalar.copy(
                out=grouped[:].rearrange("p (i q) j -> p q i j", i=PACK),
                in_=raw.rearrange("p j (q i) -> p q i j", i=PACK),
            )
            return quantise(grouped, name)

        def quantise_w2(raw, name):
            grouped = ring.tile([P, PASS, PACK], BF16, name="w_grouped", tag="w_grouped", align_bytes=64)
            nc.scalar.copy(out=grouped[:], in_=raw.rearrange("p j c -> p c j"))
            return quantise(grouped, name)

        nc.sync.dma_start(idx[:], offs)
        wf_raw = keep.tile([P, 4 * H], U8, name="wf_raw", align_bytes=64)
        nc.sync.dma_start(
            out=wf_raw[:].bitcast(I32).rearrange("p (a c) -> p a c", a=2),
            in_=wf_words.rearrange("a p c -> p a c").bitcast(I32),
        )
        for r in range(4):
            nc.sync.dma_start(
                out=tab_sc[r:P:16, :].bitcast(I32),
                in_=tab_scales[:, r:16:4, :].rearrange("a q t -> q a t").bitcast(I32),
            )
        w1_first = stage([P, 2, PACK, PASS], F32, "w1_first")
        w1_raw = {(0, 0): load_w1(w1_first, 0, 0)}
        w1_raw[1, 0] = load_w1(w1_first, 1, 0)
        tab_w = [load_table(0)]
        for r in range(4):
            nc.sync.dma_start(
                out=wf_sc_raw[r:P:32, :].bitcast(I32).rearrange("q (a t) -> q a t", a=2),
                in_=wf_scales[:, r:16:4, :].rearrange("a q t -> q a t").bitcast(I32),
            )
        tab_w.append(load_table(1))
        wgs_sb = keep.tile([P, S], F32, name="wgs_sb")
        nc.sync.dma_start(idx2[:], offs2)
        nc.sync.dma_start(out=wgs_sb[:], in_=wgs)
        nc.sync.dma_start(idx3[:], offs3)
        gain_sb = keep.tile([P, 2, PACK], F32, name="gain_sb")
        nc.sync.dma_start(out=gain_sb[:], in_=gain.rearrange("(b p i) -> p b i", b=2, i=PACK))
        bias_sb = keep.tile([P, N // P], F32, name="bias_sb")
        with nc.allow_non_contiguous_dma("bias one element a partition"):
            nc.sync.dma_start(out=bias_sb[:], in_=bias.rearrange("(t p) -> p t", p=P))

        v_w = [keep.tile([P, S], U32, name="v_w%d" % a, align_bytes=64) for a in range(2)]
        nc.vector.tensor_copy(v_sc[0][:], tab_sc[:].indirect(idx[:]))
        nc.gpsimd.dma_start(out=v_sc[1][0 : P - 16, :].bitcast(I32), in_=v_sc[0][16:P, :].bitcast(I32))
        w1_q = {(0, 0): quantise_w1(w1_raw[0, 0], "w1_00")}
        wf_w = keep.tile([P, 4, PACK, 2 * P], U8, name="wf_w", align_bytes=64)
        wf_sc = keep.tile([P, 4, PACK, P], U8, name="wf_sc", align_bytes=64)
        nc.vector.tensor_copy(
            out=wf_w[:].bitcast(U16),
            in_=wf_raw[:].bitcast(U16).rearrange("p (g q i) -> p g i q", g=4, i=PACK),
        )
        w1_q[1, 0] = quantise_w1(w1_raw[1, 0], "w1_10")
        nc.vector.tensor_copy(v_w[0][:], tab_w[0][:].bitcast(U32).indirect(idx[:]))
        nc.vector.tensor_copy(out=wf_sc[:], in_=wf_sc_raw[:].rearrange("p (g q i) -> p g i q", g=4, i=PACK))
        for start, width in RUNS:
            nc.vector.tensor_copy(
                v_w[1][:, start : start + width], tab_w[1][:].bitcast(U32).indirect(entries(idx, start, width))
            )

        ground_sb = [load_ground(0)]
        w1_second = stage([P, 2, PACK, PASS], F32, "w1_second")
        for a in range(2):
            w1_raw[a, 1] = load_w1(w1_second, a, 1)
        ground_sb.append(load_ground(1))

        def ground_rows(s):
            return ground_sb[s // PACK][:, s % PACK, :]

        h_first = [keep.tile([P, S], F32, name="h_first%d" % s) for s in range(2)]

        def h_rows(s):
            return h_first[s][:] if s < 2 else ground_rows(s - 2)

        def products(s, runs):
            b, i = divmod(s, PACK)
            made = []
            for start, width in runs:
                cols = slice(start, start + width)
                near = psum.tile([P, width], F32, name="near", tag="near", bufs=2)
                far = psum.tile([P, width], F32, name="far", tag="far", bufs=6)
                for a in range(2):
                    codes, scales = w1_q[a, b]
                    nc.tensor.matmul_mx(
                        out=near[:],
                        lhsT=codes[:, i * P : (i + 1) * P].bitcast(FP8X4),
                        lhsT_scale=scales[:, i * P : (i + 1) * P],
                        rhs=v_w[a][:, cols].bitcast(FP8X4),
                        rhs_scale=v_sc[a][:, cols],
                        start=(a == 0),
                        stop=(a == 1),
                    )
                for a in range(2):
                    nc.tensor.matmul_mx(
                        out=far[:],
                        lhsT=wf_w[:, 2 * a + b, i, :].bitcast(FP4X4),
                        lhsT_scale=wf_sc[:, 2 * a + b, i, :],
                        rhs=v_w[a][:, cols].bitcast(FP8X4),
                        rhs_scale=v_sc[a][:, cols],
                        start=(a == 0),
                        stop=(a == 1),
                    )
                near_sb = ring.tile([P, width], F32, name="near_sb", tag="near_sb", bufs=6)
                nc.scalar.copy(out=near_sb[:], in_=near[:])
                made.append((start, width, near_sb, far))
            return made

        def stronger(s, start, width, near_sb, far):
            nc.vector.tensor_tensor(h_rows(s)[:, start : start + width], far[:], near_sb[:], ALU.max)

        def place(s, start, width):
            cols = slice(start, start + width)
            nc.vector.tensor_tensor(
                pages[s % 2][:].indirect(entries(idx2, start, width)), h_rows(s)[:, cols], wgs_sb[:, cols], ALU.mult
            )

        z_grouped = [keep.tile([P, M, PACK], BF16, name="z_grouped%d" % b, align_bytes=64) for b in range(2)]

        def fetch(s, start, width):
            b, i = divmod(s, PACK)
            cols = slice(start, start + width)
            x = ring.tile([P, width], F32, name="x", tag="x", bufs=4)
            nc.vector.tensor_tensor(
                x[:], pages[s % 2][:].indirect(entries(idx3, start, width)), ground_rows(s)[:, cols], ALU.add
            )

            bounded = ring.tile([P, width], F32, name="bounded", tag="bounded")
            nc.scalar.activation(bounded[:], x[:], ACT.Tanh)
            nc.scalar.activation(z_grouped[b][:, cols, i], bounded[:], ACT.Copy, scale=gain_sb[:, b, i : i + 1])

        z_codes = [keep.tile([P, M], U32, name="z_codes%d" % b, align_bytes=64) for b in range(2)]
        z_sc = [keep.tile([P, M], U8, name="z_sc%d" % b, align_bytes=64) for b in range(2)]

        def quantise_z(b, start, width):
            cols = slice(start, start + width)
            nc.vector.quantize_mx(
                out=z_codes[b][:, cols].bitcast(FP8X4),
                scales=z_sc[b][:, cols],
                in_=z_grouped[b][:, cols, :].rearrange("p c j -> p (c j)"),
            )


        w2_q = {}
        waiting = [products(0, FIRST_RUNS), products(1, RUNS)]
        for s in range(SLICES):
            if s + 2 < SLICES:
                waiting.append(products(s + 2, RUNS))
            made = waiting[s]
            if s == 0:
                for run in made:
                    stronger(s, *run)
                    place(s, run[0], run[1])
            else:
                for run in made:
                    stronger(s, *run)
                fetch(s - 1, 0, M)
                place(s, 0, S)
            if s < 2:
                w1_q[s, 1] = quantise_w1(w1_raw[s, 1], "w1_%d1" % s)
            if s == 1:
                w2_raw = stage([P, 2, PACK, N], F32, "w2_raw")
                for b in range(2):
                    load_weight(w2_raw[:, b, :, :], w2[b * PASS : (b + 1) * PASS, :])
            if s in (4, 5):
                b = s - 4
                w2_q[b] = quantise_w2(w2_raw[:, b, :, :], "w2_%d" % b)
            if s == 5:
                quantise_z(0, 0, M)

        def product_pass(acc, b, quarter, pair):
            cols = slice(quarter * QUARTER, (quarter + 1) * QUARTER)
            codes, scales = w2_q[b]
            for u in range(2):
                t = 2 * pair + u
                nc.tensor.matmul_mx(
                    out=acc[:, u * QUARTER : (u + 1) * QUARTER],
                    lhsT=codes[:, t * P : (t + 1) * P].bitcast(FP8X4),
                    lhsT_scale=scales[:, t * P : (t + 1) * P],
                    rhs=z_codes[b][:, cols].bitcast(FP8X4),
                    rhs_scale=z_sc[b][:, cols],
                    start=(b == 0 and u == 0),
                    stop=(b == 1 and u == 1),
                )

        y = {}
        for quarter in range(4):
            for pair in range(2):
                y[quarter, pair] = psum.tile([P, BANK], F32, name="y", tag="near" if quarter == 0 else "far", bufs=2 if quarter == 0 else 6)
                product_pass(y[quarter, pair], 0, quarter, pair)

        out_view = out.rearrange("(t p) m -> p t m", p=P)
        for quarter in range(4):
            fetch(SLICES - 1, quarter * QUARTER, QUARTER)
        for quarter in range(4):
            cols = slice(quarter * QUARTER, (quarter + 1) * QUARTER)
            quantise_z(1, quarter * QUARTER, QUARTER)
            for pair in range(2):
                acc = y[quarter, pair]
                product_pass(acc, 1, quarter, pair)
                staged = keep.tile([P, 2, QUARTER], F32, name="staged%d%d" % (quarter, pair))
                for u in range(2):
                    t = 2 * pair + u
                    if pair == 1 and quarter >= 1:
                        nc.scalar.activation(
                            staged[:, u, :], acc[:, u * QUARTER : (u + 1) * QUARTER], ACT.Identity,
                            bias=bias_sb[:, t : t + 1],
                        )
                    else:
                        nc.vector.tensor_scalar(
                            staged[:, u, :], acc[:, u * QUARTER : (u + 1) * QUARTER],
                            bias_sb[:, t : t + 1], None, ALU.add,
                        )
                nc.sync.dma_start(out=out_view[:, 2 * pair : 2 * pair + 2, cols], in_=staged[:])
